import numpy as np
import ml_dtypes


def mxq(x, axis, fmt="e4m3"):
    dtype, down = {"e4m3": (ml_dtypes.float8_e4m3fn, 7), "e5m2": (ml_dtypes.float8_e5m2, 14)}[fmt]
    v = np.moveaxis(np.asarray(x, np.float32).astype(ml_dtypes.bfloat16).astype(np.float64), axis, -1)
    blocks = v.reshape(v.shape[:-1] + (-1, 32))
    amax = np.abs(blocks).max(-1, keepdims=True)
    byte = np.maximum(np.where(amax > 0, np.frexp(amax)[1] - 1 + 127, 0) - down, 1)
    scale = np.exp2(byte - 127.0)
    codes = (blocks / scale).astype(np.float32).astype(dtype).astype(np.float64)
    return np.moveaxis((codes * scale).reshape(v.shape), -1, axis)


WIDE = False


def mx_kscale(k):
    if not WIDE:
        return np.ones(k)
    levels = np.array([10, -10, 5, -5, 0])
    if k % 512:
        return np.exp2(np.random.permutation(np.resize(levels, k // 32))).repeat(32)
    a = np.empty((k // 512, 16))
    for p in range(k // 512):
        a[p, :8] = np.random.permutation(np.resize(levels, 8))
        for g in range(8):
            far = levels[np.abs(levels - a[p, g]) >= 10]
            a[p, g + 8] = far[np.random.randint(len(far))]
    return np.exp2(a.ravel()).repeat(32)


def f64(x):
    return np.asarray(x).astype(np.float64)


def striped(idx):
    return np.tile(idx.reshape(-1, 16).T, (8, 1)).astype(np.uint16)


def unstriped(offs):
    return offs[:16].T.reshape(-1).astype(np.int64)


def silu(v):
    return v / (1.0 + np.exp(-np.maximum(v, -700.0)))


K, T, E, C, N = 512, 3072, 12, 128, 512


def by_expert(wq, xq):
    return np.concatenate([wq[e].T @ xq[:, e * C:(e + 1) * C] for e in range(E)], axis=1)


def setup_inputs():
    n = np.random.standard_normal
    s = mx_kscale(K)[:, None]
    return {
        "xT": (n((K, T)) * s).astype(np.float32),
        "w": (n((E, K, N)) / np.sqrt(K) / s[None]).astype(np.float32),
        "b": (0.3 * n((N, E))).astype(np.float32),
        "gate": np.tile(np.random.uniform(0.2, 1.0, E * C), (N, 1)).astype(np.float32),
        "offs": striped(np.random.permutation(T)[:E * C]),
        "dst": striped(np.random.permutation(T)[:E * C]),
    }


def reference(xT, w, b, gate, offs, dst):
    idx = unstriped(offs)
    xq = mxq(f64(xT)[:, idx], 0, "e4m3")
    y = by_expert(mxq(f64(w), 1, "e4m3"), xq)
    y = silu(y + np.repeat(f64(b), C, axis=1))
    out = np.zeros((N, T))
    out[:, unstriped(dst)] = f64(gate) * y
    return out

@@ -1,0 +1,195 @@
+from contextlib import ExitStack
+
+import concourse.mybir as mybir
+
+K, T, E, C, N = 512, 3072, 12, 128, 512
+S = E * C
+P = 128
+J = 4
+NT = N // P
+HALF = N // 2
+G = 3
+XC = 512
+
+FLOPS = 2 * S * K * N
+BYTES = 4 * (K * T + E * K * N + N * E + S + N * T) + 2 * 2 * S
+
+F32 = mybir.dt.float32
+BF16 = mybir.dt.bfloat16
+U32 = mybir.dt.uint32
+U16 = mybir.dt.uint16
+U8 = mybir.dt.uint8
+FP8X4 = mybir.dt.float8_e4m3fn_x4
+MULT = mybir.AluOpType.mult
+SILU = mybir.ActivationFunctionType.Silu
+COPY = mybir.ActivationFunctionType.Copy
+
+
+def tile_moe_two_lin_silu_kernel(tc, xT, w, b, gate, offs, dst, out):
+    nc = tc.nc
+    with ExitStack() as ctx:
+        keep = ctx.enter_context(tc.tile_pool(name="keep", bufs=1))
+        stream = ctx.enter_context(tc.tile_pool(name="stream", bufs=4))
+        psum = ctx.enter_context(tc.psum_pool(name="psum", bufs=8))
+
+        offs_sb = keep.tile([P, S // 16], U16, name="offs_sb")
+        dst_sb = keep.tile([P, S // 16], U16, name="dst_sb")
+        planes = [stream.tile([P, T], F32, name="raw", bufs=6) for j in range(J)]
+        wins = [keep.tile([P, T], F32, name=f"win{n}") for n in range(NT)]
+        picked = [keep.tile([P, 2, S], F32, name=f"picked{u}") for u in range(2)]
+        bias = keep.tile([P, NT, E], F32, name="bias")
+        gate_sb = keep.tile([P, S], F32, name="gate_sb")
+        x_codes = keep.tile([P, S], U32, name="x_codes", align_bytes=64)
+        x_scales = keep.tile([P, S], U8, name="x_scales", align_bytes=64)
+        warm = keep.tile([P, 1], F32, name="warm")
+
+        nc.sync.dma_start(offs_sb[:], offs)
+        xk = xT.rearrange("(p j) t -> p j t", j=J)
+        for j in range(J):
+            nc.sync.dma_start(out=planes[j][:], in_=xk[:, j, :])
+        nc.scalar.dma_start(out=bias[:], in_=b.rearrange("(t p) e -> p t e", p=P))
+        nc.sync.dma_start(dst_sb[:], dst)
+
+        nc.gpsimd.memset(warm[:], 0.0)
+        nc.scalar.activation(warm[:], warm[:], SILU)
+        nc.vector.memset(wins[0][:], 0.0)
+        for n in range(1, NT):
+            nc.gpsimd.memset(wins[n][:], 0.0)
+
+        def load_w_half(raw, e, h):
+            nc.sync.dma_start(out=raw[:, e], in_=w[e, :, h * HALF:(h + 1) * HALF].rearrange("(p j) n -> p j n", j=J))
+            return raw[:, e]
+
+        def load_w(e):
+            raw = stream.tile([P, J, N], F32, name="raw", bufs=6)
+            nc.sync.dma_start(out=raw[:], in_=w[e].rearrange("(p j) n -> p j n", j=J))
+            return raw[:]
+
+        def load_gate(g):
+            cols = slice(g * G * C, (g + 1) * G * C)
+            nc.sync.dma_start(out=gate_sb[:, cols], in_=gate[0:P, cols])
+
+        def group_w(raw, width, tag, on_vector=False):
+            grouped = stream.tile([P, width, J], BF16, name=tag, bufs=3 if tag == "w_half_grouped" else 6, align_bytes=64)
+            o = grouped[:].rearrange("p (c i) j -> p c j i", i=4)
+            s = raw.rearrange("p j (c i) -> p c j i", i=4)
+            if on_vector:
+                nc.vector.tensor_copy(o, s)
+            else:
+                nc.scalar.copy(o, s)
+            return grouped
+
+        def quantize_w(grouped, codes, scales):
+            nc.vector.quantize_mx(out=codes.bitcast(FP8X4), scales=scales, in_=grouped[:].rearrange("p n j -> p (n j)"))
+
+        def code_tiles():
+            codes = stream.tile([P, N], U32, name="w_codes", bufs=6, align_bytes=64)
+            scales = stream.tile([P, N], U8, name="w_scales", bufs=6, align_bytes=64)
+            return codes, scales
+
+        for j in range(3):
+            nc.vector.tensor_copy(picked[j // 2][:, j % 2, :], planes[j][:].indirect(offs_sb[:]))
+        grouped_x = [keep.tile([P, XC, J], BF16, name=f"x_grouped{c}", align_bytes=64) for c in range(S // XC)]
+
+        def pair(c, u):
+            nc.scalar.copy(
+                grouped_x[c][:, :, 2 * u:2 * u + 2],
+                picked[u][:, :, c * XC:(c + 1) * XC].rearrange("p j s -> p s j"),
+            )
+
+        for c in range(S // XC):
+            pair(c, 0)
+        w_raw = {}
+        for h in range(2):
+            first = stream.tile([P, G, J, HALF], F32, name="raw", bufs=6)
+            for e in range(G):
+                w_raw[e, h] = load_w_half(first, e, h)
+            load_gate(h)
+        for e in range(G, E):
+            if e % G == 0 and e > G:
+                load_gate(e // G)
+            w_raw[e] = load_w(e)
+
+        def last_plane(c):
+            nc.vector.tensor_copy(picked[1][:, 1, c * XC:(c + 1) * XC], planes[3][:].indirect(offs_sb[:, c * XC // 16:(c + 1) * XC // 16]))
+            pair(c, 1)
+
+        def quantize_x(c):
+            nc.vector.quantize_mx(
+                out=x_codes[:, c * XC:(c + 1) * XC].bitcast(FP8X4),
+                scales=x_scales[:, c * XC:(c + 1) * XC],
+                in_=grouped_x[c][:].rearrange("p s j -> p (s j)"),
+            )
+
+        groups = E // G
+        grouped_w = {}
+        coded_w = {}
+        ys = {}
+
+        def stage_group(g):
+            if g < groups:
+                grouped_w[g] = [group_w(w_raw[g * G + i], N, "w_grouped") for i in range(G)]
+
+        def stage_quantize(g):
+            if g < groups:
+                coded_w[g] = [code_tiles() for i in range(G)]
+                for i, t in enumerate(grouped_w.pop(g)):
+                    codes, scales = coded_w[g][i]
+                    quantize_w(t, codes[:], scales[:])
+
+        def multiply(g, n):
+            bank = psum.tile([P, G * C], F32, name="bank")
+            y = stream.tile([P, G * C], F32, name="y", bufs=8)
+            for i in range(G):
+                e = g * G + i
+                codes, scales = coded_w[g][i]
+                nc.tensor.matmul_mx(
+                    out=bank[:, i * C:(i + 1) * C],
+                    lhsT=codes[:, n * P:(n + 1) * P].bitcast(FP8X4),
+                    lhsT_scale=scales[:, n * P:(n + 1) * P],
+                    rhs=x_codes[:, e * C:(e + 1) * C].bitcast(FP8X4),
+                    rhs_scale=x_scales[:, e * C:(e + 1) * C],
+                    start=True,
+                    stop=True,
+                )
+                nc.scalar.activation(y[:, i * C:(i + 1) * C], bank[:, i * C:(i + 1) * C], SILU, bias=bias[:, n, e:e + 1])
+            ys[g, n] = y
+
+        def stage_multiply(g):
+            if g < groups:
+                for n in range(NT):
+                    multiply(g, n)
+
+        def scatter(g, n):
+            cols = slice(g * G * C, (g + 1) * G * C)
+            nc.vector.tensor_tensor(
+                wins[n][:].indirect(dst_sb[:, g * G * C // 16:(g + 1) * G * C // 16]), ys.pop((g, n))[:], gate_sb[:, cols], MULT
+            )
+            if g == groups - 1:
+                nc.sync.dma_start(out=out[n * P:(n + 1) * P, :], in_=wins[n][:])
+
+        last_plane(0)
+        coded_w[0] = [code_tiles() for i in range(G)]
+        for h in range(2):
+            cols = slice(h * HALF, (h + 1) * HALF)
+            halves = [group_w(w_raw[i, h], HALF, "w_half_grouped", h == 0 and i == 1) for i in range(G)]
+            if h == 0:
+                quantize_x(0)
+            for i in range(G):
+                codes, scales = coded_w[0][i]
+                quantize_w(halves[i], codes[:, cols], scales[:, cols])
+            for n in range(2 * h, 2 * h + 2):
+                multiply(0, n)
+            if h == 0:
+                last_plane(1)
+        last_plane(2)
+        stage_group(1)
+        quantize_x(1)
+        for g in range(groups):
+            stage_quantize(g + 1)
+            stage_multiply(g + 1)
+            for n in range(NT):
+                scatter(g, n)
+            if g == 0:
+                quantize_x(2)
+            stage_group(g + 2)

@@ -9,7 +9,7 @@ J = 4
 NT = N // P
 HALF = N // 2
 G = 3
-XC = 512
+TC = 512
 
 FLOPS = 2 * S * K * N
 BYTES = 4 * (K * T + E * K * N + N * E + S + N * T) + 2 * 2 * S
@@ -34,34 +34,40 @@ def tile_moe_two_lin_silu_kernel(tc, xT, w, b, gate, offs, dst, out):
 
         offs_sb = keep.tile([P, S // 16], U16, name="offs_sb")
         dst_sb = keep.tile([P, S // 16], U16, name="dst_sb")
-        planes = [stream.tile([P, T], F32, name="raw", bufs=6) for j in range(J)]
         wins = [keep.tile([P, T], F32, name=f"win{n}") for n in range(NT)]
-        picked = [keep.tile([P, 2, S], F32, name=f"picked{u}") for u in range(2)]
         bias = keep.tile([P, NT, E], F32, name="bias")
         gate_sb = keep.tile([P, S], F32, name="gate_sb")
-        x_codes = keep.tile([P, S], U32, name="x_codes", align_bytes=64)
-        x_scales = keep.tile([P, S], U8, name="x_scales", align_bytes=64)
+        t_codes = keep.tile([P, T], U32, name="t_codes", align_bytes=64)
+        t_scales = keep.tile([P, T], U8, name="t_scales", align_bytes=64)
         warm = keep.tile([P, 1], F32, name="warm")
 
-        nc.sync.dma_start(offs_sb[:], offs)
         xk = xT.rearrange("(p j) t -> p j t", j=J)
-        for j in range(J):
-            nc.sync.dma_start(out=planes[j][:], in_=xk[:, j, :])
+        chunks = []
+        for c in range(T // TC):
+            raw = stream.tile([P, J, TC], F32, name="raw", bufs=10)
+            nc.sync.dma_start(out=raw[:], in_=xk[:, :, c * TC:(c + 1) * TC])
+            chunks.append(raw)
+            if c == 3:
+                nc.sync.dma_start(offs_sb[:], offs)
+            if c == 4:
+                nc.sync.dma_start(dst_sb[:], dst)
         nc.scalar.dma_start(out=bias[:], in_=b.rearrange("(t p) e -> p t e", p=P))
-        nc.sync.dma_start(dst_sb[:], dst)
 
         nc.gpsimd.memset(warm[:], 0.0)
         nc.scalar.activation(warm[:], warm[:], SILU)
-        nc.vector.memset(wins[0][:], 0.0)
+        nc.gpsimd.memset(t_scales[:], 0)
+        for n in range(1):
+            nc.vector.memset(wins[n][:], 0.0)
         for n in range(1, NT):
             nc.gpsimd.memset(wins[n][:], 0.0)
 
-        def load_w_half(raw, e, h):
-            nc.sync.dma_start(out=raw[:, e], in_=w[e, :, h * HALF:(h + 1) * HALF].rearrange("(p j) n -> p j n", j=J))
-            return raw[:, e]
+        def load_w_half(e, h):
+            raw = stream.tile([P, J, HALF], F32, name="raw", bufs=10)
+            nc.sync.dma_start(out=raw[:], in_=w[e, :, h * HALF:(h + 1) * HALF].rearrange("(p j) n -> p j n", j=J))
+            return raw[:]
 
         def load_w(e):
-            raw = stream.tile([P, J, N], F32, name="raw", bufs=6)
+            raw = stream.tile([P, J, N], F32, name="raw", bufs=10)
             nc.sync.dma_start(out=raw[:], in_=w[e].rearrange("(p j) n -> p j n", j=J))
             return raw[:]
 
@@ -69,8 +75,9 @@ def tile_moe_two_lin_silu_kernel(tc, xT, w, b, gate, offs, dst, out):
             cols = slice(g * G * C, (g + 1) * G * C)
             nc.sync.dma_start(out=gate_sb[:, cols], in_=gate[0:P, cols])
 
-        def group_w(raw, width, tag, on_vector=False):
-            grouped = stream.tile([P, width, J], BF16, name=tag, bufs=3 if tag == "w_half_grouped" else 6, align_bytes=64)
+        def interleave(raw, tag, bufs, on_vector=False):
+            width = raw.shape[2]
+            grouped = stream.tile([P, width, J], BF16, name=tag, bufs=bufs, align_bytes=64)
             o = grouped[:].rearrange("p (c i) j -> p c j i", i=4)
             s = raw.rearrange("p j (c i) -> p c j i", i=4)
             if on_vector:
@@ -79,7 +86,7 @@ def tile_moe_two_lin_silu_kernel(tc, xT, w, b, gate, offs, dst, out):
                 nc.scalar.copy(o, s)
             return grouped
 
-        def quantize_w(grouped, codes, scales):
+        def quantize(grouped, codes, scales):
             nc.vector.quantize_mx(out=codes.bitcast(FP8X4), scales=scales, in_=grouped[:].rearrange("p n j -> p (n j)"))
 
         def code_tiles():
@@ -87,39 +94,38 @@ def tile_moe_two_lin_silu_kernel(tc, xT, w, b, gate, offs, dst, out):
             scales = stream.tile([P, N], U8, name="w_scales", bufs=6, align_bytes=64)
             return codes, scales
 
-        for j in range(3):
-            nc.vector.tensor_copy(picked[j // 2][:, j % 2, :], planes[j][:].indirect(offs_sb[:]))
-        grouped_x = [keep.tile([P, XC, J], BF16, name=f"x_grouped{c}", align_bytes=64) for c in range(S // XC)]
-
-        def pair(c, u):
-            nc.scalar.copy(
-                grouped_x[c][:, :, 2 * u:2 * u + 2],
-                picked[u][:, :, c * XC:(c + 1) * XC].rearrange("p j s -> p s j"),
-            )
-
-        for c in range(S // XC):
-            pair(c, 0)
         w_raw = {}
         for h in range(2):
-            first = stream.tile([P, G, J, HALF], F32, name="raw", bufs=6)
             for e in range(G):
-                w_raw[e, h] = load_w_half(first, e, h)
+                w_raw[e, h] = load_w_half(e, h)
             load_gate(h)
         for e in range(G, E):
             if e % G == 0 and e > G:
                 load_gate(e // G)
             w_raw[e] = load_w(e)
 
-        def last_plane(c):
-            nc.vector.tensor_copy(picked[1][:, 1, c * XC:(c + 1) * XC], planes[3][:].indirect(offs_sb[:, c * XC // 16:(c + 1) * XC // 16]))
-            pair(c, 1)
+        pieces = [(0, 512, False), (512, 512, True), (1024, 512, False), (1536, 512, True), (2048, 512, False), (2560, 256, True), (2816, 256, False)]
+        ready = []
+        for t0, width, on_vector in pieces:
+            c = t0 // TC
+            grouped = interleave(chunks[c][:, :, t0 - c * TC:t0 - c * TC + width], f"x_grouped{width}", 3, on_vector)
+            ready.append((t0, width, grouped))
+            if len(ready) > 1:
+                q0, qw, grouped = ready.pop(0)
+                quantize(grouped, t_codes[:, q0:q0 + qw], t_scales[:, q0:q0 + qw])
+        for q0, qw, grouped in ready:
+            quantize(grouped, t_codes[:, q0:q0 + qw], t_scales[:, q0:q0 + qw])
 
-        def quantize_x(c):
-            nc.vector.quantize_mx(
-                out=x_codes[:, c * XC:(c + 1) * XC].bitcast(FP8X4),
-                scales=x_scales[:, c * XC:(c + 1) * XC],
-                in_=grouped_x[c][:].rearrange("p s j -> p (s j)"),
-            )
+        picked = {}
+
+        def gather(g):
+            if g < E // G:
+                picks = offs_sb[:, g * G * C // 16:(g + 1) * G * C // 16]
+                codes = stream.tile([P, G * C], U32, name="x_codes", bufs=2, align_bytes=64)
+                scales = stream.tile([P, G * C], U8, name="x_scales", bufs=2, align_bytes=64)
+                nc.vector.tensor_copy(codes[:], t_codes[:].indirect(picks))
+                nc.vector.tensor_copy(scales[:], t_scales[:].indirect(picks))
+                picked[g] = codes, scales
 
         groups = E // G
         grouped_w = {}
@@ -128,14 +134,14 @@ def tile_moe_two_lin_silu_kernel(tc, xT, w, b, gate, offs, dst, out):
 
         def stage_group(g):
             if g < groups:
-                grouped_w[g] = [group_w(w_raw[g * G + i], N, "w_grouped") for i in range(G)]
+                grouped_w[g] = [interleave(w_raw[g * G + i], "w_grouped", 6, (g * G + i) in ()) for i in range(G)]
 
         def stage_quantize(g):
             if g < groups:
                 coded_w[g] = [code_tiles() for i in range(G)]
                 for i, t in enumerate(grouped_w.pop(g)):
                     codes, scales = coded_w[g][i]
-                    quantize_w(t, codes[:], scales[:])
+                    quantize(t, codes[:], scales[:])
 
         def multiply(g, n):
             bank = psum.tile([P, G * C], F32, name="bank")
@@ -143,12 +149,13 @@ def tile_moe_two_lin_silu_kernel(tc, xT, w, b, gate, offs, dst, out):
             for i in range(G):
                 e = g * G + i
                 codes, scales = coded_w[g][i]
+                x_codes, x_scales = picked[g]
                 nc.tensor.matmul_mx(
                     out=bank[:, i * C:(i + 1) * C],
                     lhsT=codes[:, n * P:(n + 1) * P].bitcast(FP8X4),
                     lhsT_scale=scales[:, n * P:(n + 1) * P],
-                    rhs=x_codes[:, e * C:(e + 1) * C].bitcast(FP8X4),
-                    rhs_scale=x_scales[:, e * C:(e + 1) * C],
+                    rhs=x_codes[:, i * C:(i + 1) * C].bitcast(FP8X4),
+                    rhs_scale=x_scales[:, i * C:(i + 1) * C],
                     start=True,
                     stop=True,
                 )
@@ -168,28 +175,24 @@ def tile_moe_two_lin_silu_kernel(tc, xT, w, b, gate, offs, dst, out):
             if g == groups - 1:
                 nc.sync.dma_start(out=out[n * P:(n + 1) * P, :], in_=wins[n][:])
 
-        last_plane(0)
+        gather(0)
         coded_w[0] = [code_tiles() for i in range(G)]
         for h in range(2):
             cols = slice(h * HALF, (h + 1) * HALF)
-            halves = [group_w(w_raw[i, h], HALF, "w_half_grouped", h == 0 and i == 1) for i in range(G)]
-            if h == 0:
-                quantize_x(0)
+            halves = [interleave(w_raw[i, h], "w_half_grouped", 4, (i, h) in ((1, 0),)) for i in range(G)]
             for i in range(G):
                 codes, scales = coded_w[0][i]
-                quantize_w(halves[i], codes[:, cols], scales[:, cols])
+                quantize(halves[i], codes[:, cols], scales[:, cols])
             for n in range(2 * h, 2 * h + 2):
                 multiply(0, n)
             if h == 0:
-                last_plane(1)
-        last_plane(2)
+                gather(1)
         stage_group(1)
-        quantize_x(1)
         for g in range(groups):
+            if g > 0:
+                gather(g + 1)
             stage_quantize(g + 1)
             stage_multiply(g + 1)
             for n in range(NT):
                 scatter(g, n)
-            if g == 0:
-                quantize_x(2)
             stage_group(g + 2)

@@ -8,8 +8,10 @@ P = 128
 J = 4
 NT = N // P
 HALF = N // 2
-G = 3
-TC = 512
+GROUPS = (4, 4, 4)
+STARTS = (0, 4, 8, 12)
+GATE_LOADS = ((7, 0, 0, 1), (10, 0, 1, 4), (9, 1, 0, 2), (16, 1, 2, 4), (16, 2, 0, 4))
+BANK = 4
 
 FLOPS = 2 * S * K * N
 BYTES = 4 * (K * T + E * K * N + N * E + S + N * T) + 2 * 2 * S
@@ -36,130 +38,135 @@ def tile_moe_two_lin_silu_kernel(tc, xT, w, b, gate, offs, dst, out):
         dst_sb = keep.tile([P, S // 16], U16, name="dst_sb")
         wins = [keep.tile([P, T], F32, name=f"win{n}") for n in range(NT)]
         bias = keep.tile([P, NT, E], F32, name="bias")
-        gate_sb = keep.tile([P, S], F32, name="gate_sb")
         t_codes = keep.tile([P, T], U32, name="t_codes", align_bytes=64)
         t_scales = keep.tile([P, T], U8, name="t_scales", align_bytes=64)
         warm = keep.tile([P, 1], F32, name="warm")
 
         xk = xT.rearrange("(p j) t -> p j t", j=J)
         chunks = []
-        for c in range(T // TC):
-            raw = stream.tile([P, J, TC], F32, name="raw", bufs=10)
-            nc.sync.dma_start(out=raw[:], in_=xk[:, :, c * TC:(c + 1) * TC])
+        spans = [(0, 1024), (1024, 2048), (2048, 2560), (2560, 3072)]
+        for c, (t0, t1) in enumerate(spans):
+            if t1 - t0 > N:
+                raw = stream.tile([P, J, t1 - t0], F32, name="x_raw", bufs=2)
+            else:
+                raw = stream.tile([P, J, t1 - t0], F32, name="raw", bufs=6)
+            nc.sync.dma_start(out=raw[:], in_=xk[:, :, t0:t1])
             chunks.append(raw)
-            if c == 3:
+            if c == len(spans) - 2:
                 nc.sync.dma_start(offs_sb[:], offs)
-            if c == 4:
                 nc.sync.dma_start(dst_sb[:], dst)
         nc.scalar.dma_start(out=bias[:], in_=b.rearrange("(t p) e -> p t e", p=P))
 
         nc.gpsimd.memset(warm[:], 0.0)
         nc.scalar.activation(warm[:], warm[:], SILU)
         nc.gpsimd.memset(t_scales[:], 0)
-        for n in range(1):
+        for n in range(2):
             nc.vector.memset(wins[n][:], 0.0)
-        for n in range(1, NT):
+        for n in range(2, NT):
             nc.gpsimd.memset(wins[n][:], 0.0)
 
-        def load_w_half(e, h):
-            raw = stream.tile([P, J, HALF], F32, name="raw", bufs=10)
-            nc.sync.dma_start(out=raw[:], in_=w[e, :, h * HALF:(h + 1) * HALF].rearrange("(p j) n -> p j n", j=J))
-            return raw[:]
+        gates = {}
 
-        def load_w(e):
-            raw = stream.tile([P, J, N], F32, name="raw", bufs=10)
-            nc.sync.dma_start(out=raw[:], in_=w[e].rearrange("(p j) n -> p j n", j=J))
-            return raw[:]
+        def load_gate(g, n0, n1):
+            gate_sb = stream.tile([P, GROUPS[g] * C], F32, name="gate_sb", bufs=5)
+            nc.sync.dma_start(out=gate_sb[:], in_=gate[n0 * P:(n0 + 1) * P, STARTS[g] * C:STARTS[g + 1] * C])
+            for n in range(n0, n1):
+                gates[g, n] = gate_sb
 
-        def load_gate(g):
-            cols = slice(g * G * C, (g + 1) * G * C)
-            nc.sync.dma_start(out=gate_sb[:, cols], in_=gate[0:P, cols])
-
-        def interleave(raw, tag, bufs, on_vector=False):
-            width = raw.shape[2]
-            grouped = stream.tile([P, width, J], BF16, name=tag, bufs=bufs, align_bytes=64)
-            o = grouped[:].rearrange("p (c i) j -> p c j i", i=4)
+        def copy(on_vector, grouped, raw):
+            o = grouped.rearrange("p (c i) j -> p c j i", i=4)
             s = raw.rearrange("p j (c i) -> p c j i", i=4)
             if on_vector:
                 nc.vector.tensor_copy(o, s)
             else:
                 nc.scalar.copy(o, s)
-            return grouped
 
         def quantize(grouped, codes, scales):
-            nc.vector.quantize_mx(out=codes.bitcast(FP8X4), scales=scales, in_=grouped[:].rearrange("p n j -> p (n j)"))
-
-        def code_tiles():
-            codes = stream.tile([P, N], U32, name="w_codes", bufs=6, align_bytes=64)
-            scales = stream.tile([P, N], U8, name="w_scales", bufs=6, align_bytes=64)
-            return codes, scales
+            nc.vector.quantize_mx(out=codes.bitcast(FP8X4), scales=scales, in_=grouped.rearrange("p n j -> p (n j)"))
 
         w_raw = {}
-        for h in range(2):
-            for e in range(G):
-                w_raw[e, h] = load_w_half(e, h)
-            load_gate(h)
-        for e in range(G, E):
-            if e % G == 0 and e > G:
-                load_gate(e // G)
-            w_raw[e] = load_w(e)
+        items = [(e, h) for h in range(2) for e in range(GROUPS[0])] + [(e, None) for e in range(GROUPS[0], E)]
+        for k, (e, h) in enumerate(items):
+            for k0, g, n0, n1 in GATE_LOADS:
+                if k0 == k:
+                    load_gate(g, n0, n1)
+            if h is None:
+                raw = stream.tile([P, J, N], F32, name="raw", bufs=6)
+                nc.sync.dma_start(out=raw[:], in_=w[e].rearrange("(p j) n -> p j n", j=J))
+                w_raw[e] = raw[:]
+            else:
+                raw = stream.tile([P, J, HALF], F32, name="raw", bufs=6)
+                nc.sync.dma_start(out=raw[:], in_=w[e, :, h * HALF:(h + 1) * HALF].rearrange("(p j) n -> p j n", j=J))
+                w_raw[e, h] = raw[:]
+        for k0, g, n0, n1 in GATE_LOADS:
+            if k0 == len(items):
+                load_gate(g, n0, n1)
 
-        pieces = [(0, 512, False), (512, 512, True), (1024, 512, False), (1536, 512, True), (2048, 512, False), (2560, 256, True), (2816, 256, False)]
+        halves = [512, 512, 256, 256]
         ready = []
-        for t0, width, on_vector in pieces:
-            c = t0 // TC
-            grouped = interleave(chunks[c][:, :, t0 - c * TC:t0 - c * TC + width], f"x_grouped{width}", 3, on_vector)
-            ready.append((t0, width, grouped))
+        for c, (t0, t1) in enumerate(spans):
+            width = t1 - t0
+            grouped = stream.tile([P, width, J], BF16, name=f"x_grouped{width}", bufs=1, align_bytes=64)
+            cut = width - halves[c]
+            copy(False, grouped[:, 0:cut], chunks[c][:, :, 0:cut])
+            copy(True, grouped[:, cut:width], chunks[c][:, :, cut:width])
+            ready.append((grouped, t0, t1))
             if len(ready) > 1:
-                q0, qw, grouped = ready.pop(0)
-                quantize(grouped, t_codes[:, q0:q0 + qw], t_scales[:, q0:q0 + qw])
-        for q0, qw, grouped in ready:
-            quantize(grouped, t_codes[:, q0:q0 + qw], t_scales[:, q0:q0 + qw])
+                grouped, q0, q1 = ready.pop(0)
+                quantize(grouped[:], t_codes[:, q0:q1], t_scales[:, q0:q1])
+        for grouped, q0, q1 in ready:
+            quantize(grouped[:], t_codes[:, q0:q1], t_scales[:, q0:q1])
 
         picked = {}
 
-        def gather(g):
-            if g < E // G:
-                picks = offs_sb[:, g * G * C // 16:(g + 1) * G * C // 16]
-                codes = stream.tile([P, G * C], U32, name="x_codes", bufs=2, align_bytes=64)
-                scales = stream.tile([P, G * C], U8, name="x_scales", bufs=2, align_bytes=64)
-                nc.vector.tensor_copy(codes[:], t_codes[:].indirect(picks))
-                nc.vector.tensor_copy(scales[:], t_scales[:].indirect(picks))
-                picked[g] = codes, scales
+        def gather(e0, e1):
+            picks = offs_sb[:, e0 * C // 16:e1 * C // 16]
+            codes = stream.tile([P, (e1 - e0) * C], U32, name=f"x_codes{e0}", bufs=1, align_bytes=64)
+            scales = stream.tile([P, (e1 - e0) * C], U8, name=f"x_scales{e0}", bufs=1, align_bytes=64)
+            nc.vector.tensor_copy(codes[:], t_codes[:].indirect(picks))
+            nc.vector.tensor_copy(scales[:], t_scales[:].indirect(picks))
+            for e in range(e0, e1):
+                c0 = (e - e0) * C
+                picked[e] = codes[:, c0:c0 + C], scales[:, c0:c0 + C]
 
-        groups = E // G
+        groups = len(GROUPS)
         grouped_w = {}
         coded_w = {}
         ys = {}
 
         def stage_group(g):
             if g < groups:
-                grouped_w[g] = [interleave(w_raw[g * G + i], "w_grouped", 6, (g * G + i) in ()) for i in range(G)]
+                for e in range(STARTS[g], STARTS[g + 1]):
+                    grouped = stream.tile([P, N, J], BF16, name="w_grouped", bufs=5, align_bytes=64)
+                    copy(e in (4, 5), grouped[:], w_raw[e])
+                    grouped_w[e] = grouped
 
         def stage_quantize(g):
             if g < groups:
-                coded_w[g] = [code_tiles() for i in range(G)]
-                for i, t in enumerate(grouped_w.pop(g)):
-                    codes, scales = coded_w[g][i]
-                    quantize(t, codes[:], scales[:])
+                for e in range(STARTS[g], STARTS[g + 1]):
+                    codes = stream.tile([P, N], U32, name="w_codes", bufs=8, align_bytes=64)
+                    scales = stream.tile([P, N], U8, name="w_scales", bufs=8, align_bytes=64)
+                    quantize(grouped_w[e][:], codes[:], scales[:])
+                    for n in range(NT):
+                        coded_w[e, n] = codes[:, n * P:(n + 1) * P], scales[:, n * P:(n + 1) * P]
 
         def multiply(g, n):
-            bank = psum.tile([P, G * C], F32, name="bank")
-            y = stream.tile([P, G * C], F32, name="y", bufs=8)
-            for i in range(G):
-                e = g * G + i
-                codes, scales = coded_w[g][i]
-                x_codes, x_scales = picked[g]
+            y = stream.tile([P, GROUPS[g] * C], F32, name="y", bufs=7)
+            for i in range(GROUPS[g]):
+                e = STARTS[g] + i
+                if i % BANK == 0:
+                    bank = psum.tile([P, BANK * C], F32, name="bank")
+                acc = bank[:, i % BANK * C:(i % BANK + 1) * C]
                 nc.tensor.matmul_mx(
-                    out=bank[:, i * C:(i + 1) * C],
-                    lhsT=codes[:, n * P:(n + 1) * P].bitcast(FP8X4),
-                    lhsT_scale=scales[:, n * P:(n + 1) * P],
-                    rhs=x_codes[:, i * C:(i + 1) * C].bitcast(FP8X4),
-                    rhs_scale=x_scales[:, i * C:(i + 1) * C],
+                    out=acc,
+                    lhsT=coded_w[e, n][0].bitcast(FP8X4),
+                    lhsT_scale=coded_w[e, n][1],
+                    rhs=picked[e][0].bitcast(FP8X4),
+                    rhs_scale=picked[e][1],
                     start=True,
                     stop=True,
                 )
-                nc.scalar.activation(y[:, i * C:(i + 1) * C], bank[:, i * C:(i + 1) * C], SILU, bias=bias[:, n, e:e + 1])
+                nc.scalar.activation(y[:, i * C:(i + 1) * C], acc, SILU, bias=bias[:, n, e:e + 1])
             ys[g, n] = y
 
         def stage_multiply(g):
@@ -168,29 +175,35 @@ def tile_moe_two_lin_silu_kernel(tc, xT, w, b, gate, offs, dst, out):
                     multiply(g, n)
 
         def scatter(g, n):
-            cols = slice(g * G * C, (g + 1) * G * C)
-            nc.vector.tensor_tensor(
-                wins[n][:].indirect(dst_sb[:, g * G * C // 16:(g + 1) * G * C // 16]), ys.pop((g, n))[:], gate_sb[:, cols], MULT
-            )
+            places = dst_sb[:, STARTS[g] * C // 16:STARTS[g + 1] * C // 16]
+            nc.vector.tensor_tensor(wins[n][:].indirect(places), ys[g, n][:], gates[g, n][:], MULT)
             if g == groups - 1:
                 nc.sync.dma_start(out=out[n * P:(n + 1) * P, :], in_=wins[n][:])
 
-        gather(0)
-        coded_w[0] = [code_tiles() for i in range(G)]
+        gather(0, GROUPS[0])
+        first = []
+        for e in range(GROUPS[0]):
+            codes = stream.tile([P, N], U32, name="w_codes", bufs=8, align_bytes=64)
+            scales = stream.tile([P, N], U8, name="w_scales", bufs=8, align_bytes=64)
+            first.append((codes, scales))
         for h in range(2):
+            halved = []
+            for e in range(GROUPS[0]):
+                grouped = stream.tile([P, HALF, J], BF16, name="w_half_grouped", bufs=4, align_bytes=64)
+                copy((e, h) in ((1, 1),), grouped[:], w_raw[e, h])
+                halved.append(grouped)
             cols = slice(h * HALF, (h + 1) * HALF)
-            halves = [interleave(w_raw[i, h], "w_half_grouped", 4, (i, h) in ((1, 0),)) for i in range(G)]
-            for i in range(G):
-                codes, scales = coded_w[0][i]
-                quantize(halves[i], codes[:, cols], scales[:, cols])
+            for e in range(GROUPS[0]):
+                codes, scales = first[e]
+                quantize(halved[e][:], codes[:, cols], scales[:, cols])
+                for n in range(2 * h, 2 * h + 2):
+                    coded_w[e, n] = codes[:, n * P:(n + 1) * P], scales[:, n * P:(n + 1) * P]
             for n in range(2 * h, 2 * h + 2):
                 multiply(0, n)
-            if h == 0:
-                gather(1)
         stage_group(1)
         for g in range(groups):
-            if g > 0:
-                gather(g + 1)
+            if g == 0:
+                gather(GROUPS[0], E)
             stage_quantize(g + 1)
             stage_multiply(g + 1)
             for n in range(NT):

@@ -10,7 +10,8 @@ NT = N // P
 HALF = N // 2
 GROUPS = (4, 4, 4)
 STARTS = (0, 4, 8, 12)
-GATE_LOADS = ((7, 0, 0, 1), (10, 0, 1, 4), (9, 1, 0, 2), (16, 1, 2, 4), (16, 2, 0, 4))
+GATE_LOADS = ((2, 0, 0, 2), (11, 0, 2, 4), (14, 1, 0, 3), (16, 1, 3, 4), (16, 2, 0, 4))
+PAIR = 2
 BANK = 4
 
 FLOPS = 2 * S * K * N
@@ -49,12 +50,11 @@ def tile_moe_two_lin_silu_kernel(tc, xT, w, b, gate, offs, dst, out):
             if t1 - t0 > N:
                 raw = stream.tile([P, J, t1 - t0], F32, name="x_raw", bufs=2)
             else:
-                raw = stream.tile([P, J, t1 - t0], F32, name="raw", bufs=6)
+                raw = stream.tile([P, J, t1 - t0], F32, name="raw", bufs=5)
             nc.sync.dma_start(out=raw[:], in_=xk[:, :, t0:t1])
             chunks.append(raw)
-            if c == len(spans) - 2:
-                nc.sync.dma_start(offs_sb[:], offs)
-                nc.sync.dma_start(dst_sb[:], dst)
+        nc.sync.dma_start(offs_sb[:], offs)
+        nc.sync.dma_start(dst_sb[:], dst)
         nc.scalar.dma_start(out=bias[:], in_=b.rearrange("(t p) e -> p t e", p=P))
 
         nc.gpsimd.memset(warm[:], 0.0)
@@ -68,7 +68,7 @@ def tile_moe_two_lin_silu_kernel(tc, xT, w, b, gate, offs, dst, out):
         gates = {}
 
         def load_gate(g, n0, n1):
-            gate_sb = stream.tile([P, GROUPS[g] * C], F32, name="gate_sb", bufs=5)
+            gate_sb = stream.tile([P, GROUPS[g] * C], F32, name="gate_sb", bufs=4)
             nc.sync.dma_start(out=gate_sb[:], in_=gate[n0 * P:(n0 + 1) * P, STARTS[g] * C:STARTS[g + 1] * C])
             for n in range(n0, n1):
                 gates[g, n] = gate_sb
@@ -91,11 +91,11 @@ def tile_moe_two_lin_silu_kernel(tc, xT, w, b, gate, offs, dst, out):
                 if k0 == k:
                     load_gate(g, n0, n1)
             if h is None:
-                raw = stream.tile([P, J, N], F32, name="raw", bufs=6)
+                raw = stream.tile([P, J, N], F32, name="raw", bufs=5)
                 nc.sync.dma_start(out=raw[:], in_=w[e].rearrange("(p j) n -> p j n", j=J))
                 w_raw[e] = raw[:]
             else:
-                raw = stream.tile([P, J, HALF], F32, name="raw", bufs=6)
+                raw = stream.tile([P, J, HALF], F32, name="raw", bufs=5)
                 nc.sync.dma_start(out=raw[:], in_=w[e, :, h * HALF:(h + 1) * HALF].rearrange("(p j) n -> p j n", j=J))
                 w_raw[e, h] = raw[:]
         for k0, g, n0, n1 in GATE_LOADS:
@@ -137,21 +137,22 @@ def tile_moe_two_lin_silu_kernel(tc, xT, w, b, gate, offs, dst, out):
         def stage_group(g):
             if g < groups:
                 for e in range(STARTS[g], STARTS[g + 1]):
-                    grouped = stream.tile([P, N, J], BF16, name="w_grouped", bufs=5, align_bytes=64)
-                    copy(e in (4, 5), grouped[:], w_raw[e])
+                    if e % PAIR == 0:
+                        grouped = stream.tile([P, PAIR, N, J], BF16, name="w_grouped", bufs=2, align_bytes=64)
+                    copy(e in (7,), grouped[:, e % PAIR], w_raw[e])
                     grouped_w[e] = grouped
 
         def stage_quantize(g):
             if g < groups:
-                for e in range(STARTS[g], STARTS[g + 1]):
-                    codes = stream.tile([P, N], U32, name="w_codes", bufs=8, align_bytes=64)
-                    scales = stream.tile([P, N], U8, name="w_scales", bufs=8, align_bytes=64)
-                    quantize(grouped_w[e][:], codes[:], scales[:])
-                    for n in range(NT):
-                        coded_w[e, n] = codes[:, n * P:(n + 1) * P], scales[:, n * P:(n + 1) * P]
+                for e in range(STARTS[g], STARTS[g + 1], PAIR):
+                    codes = stream.tile([P, PAIR * N], U32, name="w_codes", bufs=3, align_bytes=64)
+                    scales = stream.tile([P, PAIR * N], U8, name="w_scales", bufs=3, align_bytes=64)
+                    quantize(grouped_w[e][:].rearrange("p e n j -> p (e n) j"), codes[:], scales[:])
+                    for k in range(PAIR * NT):
+                        coded_w[e + k // NT, k % NT] = codes[:, k * P:(k + 1) * P], scales[:, k * P:(k + 1) * P]
 
         def multiply(g, n):
-            y = stream.tile([P, GROUPS[g] * C], F32, name="y", bufs=7)
+            y = stream.tile([P, GROUPS[g] * C], F32, name="y", bufs=6)
             for i in range(GROUPS[g]):
                 e = STARTS[g] + i
                 if i % BANK == 0:
@@ -180,30 +181,22 @@ def tile_moe_two_lin_silu_kernel(tc, xT, w, b, gate, offs, dst, out):
             if g == groups - 1:
                 nc.sync.dma_start(out=out[n * P:(n + 1) * P, :], in_=wins[n][:])
 
-        gather(0, GROUPS[0])
-        first = []
-        for e in range(GROUPS[0]):
-            codes = stream.tile([P, N], U32, name="w_codes", bufs=8, align_bytes=64)
-            scales = stream.tile([P, N], U8, name="w_scales", bufs=8, align_bytes=64)
-            first.append((codes, scales))
+        gather(0, E)
         for h in range(2):
-            halved = []
+            halved = stream.tile([P, GROUPS[0], HALF, J], BF16, name="w_halved", bufs=2, align_bytes=64)
             for e in range(GROUPS[0]):
-                grouped = stream.tile([P, HALF, J], BF16, name="w_half_grouped", bufs=4, align_bytes=64)
-                copy((e, h) in ((1, 1),), grouped[:], w_raw[e, h])
-                halved.append(grouped)
-            cols = slice(h * HALF, (h + 1) * HALF)
+                copy((e, h) in ((1, 1), (2, 1)), halved[:, e], w_raw[e, h])
+            codes = stream.tile([P, GROUPS[0] * HALF], U32, name="w_half_codes", bufs=2, align_bytes=64)
+            scales = stream.tile([P, GROUPS[0] * HALF], U8, name="w_half_scales", bufs=2, align_bytes=64)
+            quantize(halved[:].rearrange("p e n j -> p (e n) j"), codes[:], scales[:])
             for e in range(GROUPS[0]):
-                codes, scales = first[e]
-                quantize(halved[e][:], codes[:, cols], scales[:, cols])
-                for n in range(2 * h, 2 * h + 2):
-                    coded_w[e, n] = codes[:, n * P:(n + 1) * P], scales[:, n * P:(n + 1) * P]
+                for m in range(2):
+                    c0 = e * HALF + m * P
+                    coded_w[e, 2 * h + m] = codes[:, c0:c0 + P], scales[:, c0:c0 + P]
             for n in range(2 * h, 2 * h + 2):
                 multiply(0, n)
         stage_group(1)
         for g in range(groups):
-            if g == 0:
-                gather(GROUPS[0], E)
             stage_quantize(g + 1)
             stage_multiply(g + 1)
             for n in range(NT):

@@ -60,10 +60,8 @@ def tile_moe_two_lin_silu_kernel(tc, xT, w, b, gate, offs, dst, out):
         nc.gpsimd.memset(warm[:], 0.0)
         nc.scalar.activation(warm[:], warm[:], SILU)
         nc.gpsimd.memset(t_scales[:], 0)
-        for n in range(2):
-            nc.vector.memset(wins[n][:], 0.0)
-        for n in range(2, NT):
-            nc.gpsimd.memset(wins[n][:], 0.0)
+        for win in wins:
+            nc.vector.memset(win[:], 0.0)
 
         gates = {}
 
@@ -102,7 +100,7 @@ def tile_moe_two_lin_silu_kernel(tc, xT, w, b, gate, offs, dst, out):
             if k0 == len(items):
                 load_gate(g, n0, n1)
 
-        halves = [512, 512, 256, 256]
+        halves = [640, 640, 256, 256]
         ready = []
         for c, (t0, t1) in enumerate(spans):
             width = t1 - t0

from contextlib import ExitStack

import concourse.mybir as mybir

K, T, E, C, N = 512, 3072, 12, 128, 512
S = E * C
P = 128
J = 4
NT = N // P
HALF = N // 2
GROUPS = (4, 4, 4)
STARTS = (0, 4, 8, 12)
GATE_LOADS = ((2, 0, 0, 2), (11, 0, 2, 4), (14, 1, 0, 3), (16, 1, 3, 4), (16, 2, 0, 4))
PAIR = 2
BANK = 4

FLOPS = 2 * S * K * N
BYTES = 4 * (K * T + E * K * N + N * E + S + N * T) + 2 * 2 * S

F32 = mybir.dt.float32
BF16 = mybir.dt.bfloat16
U32 = mybir.dt.uint32
U16 = mybir.dt.uint16
U8 = mybir.dt.uint8
FP8X4 = mybir.dt.float8_e4m3fn_x4
MULT = mybir.AluOpType.mult
SILU = mybir.ActivationFunctionType.Silu
COPY = mybir.ActivationFunctionType.Copy


def tile_moe_two_lin_silu_kernel(tc, xT, w, b, gate, offs, dst, out):
    nc = tc.nc
    with ExitStack() as ctx:
        keep = ctx.enter_context(tc.tile_pool(name="keep", bufs=1))
        stream = ctx.enter_context(tc.tile_pool(name="stream", bufs=4))
        psum = ctx.enter_context(tc.psum_pool(name="psum", bufs=8))

        offs_sb = keep.tile([P, S // 16], U16, name="offs_sb")
        dst_sb = keep.tile([P, S // 16], U16, name="dst_sb")
        wins = [keep.tile([P, T], F32, name=f"win{n}") for n in range(NT)]
        bias = keep.tile([P, NT, E], F32, name="bias")
        t_codes = keep.tile([P, T], U32, name="t_codes", align_bytes=64)
        t_scales = keep.tile([P, T], U8, name="t_scales", align_bytes=64)
        warm = keep.tile([P, 1], F32, name="warm")

        xk = xT.rearrange("(p j) t -> p j t", j=J)
        chunks = []
        spans = [(0, 1024), (1024, 2048), (2048, 2560), (2560, 3072)]
        for c, (t0, t1) in enumerate(spans):
            if t1 - t0 > N:
                raw = stream.tile([P, J, t1 - t0], F32, name="x_raw", bufs=2)
            else:
                raw = stream.tile([P, J, t1 - t0], F32, name="raw", bufs=5)
            nc.sync.dma_start(out=raw[:], in_=xk[:, :, t0:t1])
            chunks.append(raw)
        nc.sync.dma_start(offs_sb[:], offs)
        nc.sync.dma_start(dst_sb[:], dst)
        nc.scalar.dma_start(out=bias[:], in_=b.rearrange("(t p) e -> p t e", p=P))

        nc.gpsimd.memset(warm[:], 0.0)
        nc.scalar.activation(warm[:], warm[:], SILU)
        nc.gpsimd.memset(t_scales[:], 0)
        for win in wins:
            nc.vector.memset(win[:], 0.0)

        gates = {}

        def load_gate(g, n0, n1):
            gate_sb = stream.tile([P, GROUPS[g] * C], F32, name="gate_sb", bufs=4)
            nc.sync.dma_start(out=gate_sb[:], in_=gate[n0 * P:(n0 + 1) * P, STARTS[g] * C:STARTS[g + 1] * C])
            for n in range(n0, n1):
                gates[g, n] = gate_sb

        def copy(on_vector, grouped, raw):
            o = grouped.rearrange("p (c i) j -> p c j i", i=4)
            s = raw.rearrange("p j (c i) -> p c j i", i=4)
            if on_vector:
                nc.vector.tensor_copy(o, s)
            else:
                nc.scalar.copy(o, s)

        def quantize(grouped, codes, scales):
            nc.vector.quantize_mx(out=codes.bitcast(FP8X4), scales=scales, in_=grouped.rearrange("p n j -> p (n j)"))

        w_raw = {}
        items = [(e, h) for h in range(2) for e in range(GROUPS[0])] + [(e, None) for e in range(GROUPS[0], E)]
        for k, (e, h) in enumerate(items):
            for k0, g, n0, n1 in GATE_LOADS:
                if k0 == k:
                    load_gate(g, n0, n1)
            if h is None:
                raw = stream.tile([P, J, N], F32, name="raw", bufs=5)
                nc.sync.dma_start(out=raw[:], in_=w[e].rearrange("(p j) n -> p j n", j=J))
                w_raw[e] = raw[:]
            else:
                raw = stream.tile([P, J, HALF], F32, name="raw", bufs=5)
                nc.sync.dma_start(out=raw[:], in_=w[e, :, h * HALF:(h + 1) * HALF].rearrange("(p j) n -> p j n", j=J))
                w_raw[e, h] = raw[:]
        for k0, g, n0, n1 in GATE_LOADS:
            if k0 == len(items):
                load_gate(g, n0, n1)

        halves = [640, 640, 256, 256]
        ready = []
        for c, (t0, t1) in enumerate(spans):
            width = t1 - t0
            grouped = stream.tile([P, width, J], BF16, name=f"x_grouped{width}", bufs=1, align_bytes=64)
            cut = width - halves[c]
            copy(False, grouped[:, 0:cut], chunks[c][:, :, 0:cut])
            copy(True, grouped[:, cut:width], chunks[c][:, :, cut:width])
            ready.append((grouped, t0, t1))
            if len(ready) > 1:
                grouped, q0, q1 = ready.pop(0)
                quantize(grouped[:], t_codes[:, q0:q1], t_scales[:, q0:q1])
        for grouped, q0, q1 in ready:
            quantize(grouped[:], t_codes[:, q0:q1], t_scales[:, q0:q1])

        picked = {}

        def gather(e0, e1):
            picks = offs_sb[:, e0 * C // 16:e1 * C // 16]
            codes = stream.tile([P, (e1 - e0) * C], U32, name=f"x_codes{e0}", bufs=1, align_bytes=64)
            scales = stream.tile([P, (e1 - e0) * C], U8, name=f"x_scales{e0}", bufs=1, align_bytes=64)
            nc.vector.tensor_copy(codes[:], t_codes[:].indirect(picks))
            nc.vector.tensor_copy(scales[:], t_scales[:].indirect(picks))
            for e in range(e0, e1):
                c0 = (e - e0) * C
                picked[e] = codes[:, c0:c0 + C], scales[:, c0:c0 + C]

        groups = len(GROUPS)
        grouped_w = {}
        coded_w = {}
        ys = {}

        def stage_group(g):
            if g < groups:
                for e in range(STARTS[g], STARTS[g + 1]):
                    if e % PAIR == 0:
                        grouped = stream.tile([P, PAIR, N, J], BF16, name="w_grouped", bufs=2, align_bytes=64)
                    copy(e in (7,), grouped[:, e % PAIR], w_raw[e])
                    grouped_w[e] = grouped

        def stage_quantize(g):
            if g < groups:
                for e in range(STARTS[g], STARTS[g + 1], PAIR):
                    codes = stream.tile([P, PAIR * N], U32, name="w_codes", bufs=3, align_bytes=64)
                    scales = stream.tile([P, PAIR * N], U8, name="w_scales", bufs=3, align_bytes=64)
                    quantize(grouped_w[e][:].rearrange("p e n j -> p (e n) j"), codes[:], scales[:])
                    for k in range(PAIR * NT):
                        coded_w[e + k // NT, k % NT] = codes[:, k * P:(k + 1) * P], scales[:, k * P:(k + 1) * P]

        def multiply(g, n):
            y = stream.tile([P, GROUPS[g] * C], F32, name="y", bufs=6)
            for i in range(GROUPS[g]):
                e = STARTS[g] + i
                if i % BANK == 0:
                    bank = psum.tile([P, BANK * C], F32, name="bank")
                acc = bank[:, i % BANK * C:(i % BANK + 1) * C]
                nc.tensor.matmul_mx(
                    out=acc,
                    lhsT=coded_w[e, n][0].bitcast(FP8X4),
                    lhsT_scale=coded_w[e, n][1],
                    rhs=picked[e][0].bitcast(FP8X4),
                    rhs_scale=picked[e][1],
                    start=True,
                    stop=True,
                )
                nc.scalar.activation(y[:, i * C:(i + 1) * C], acc, SILU, bias=bias[:, n, e:e + 1])
            ys[g, n] = y

        def stage_multiply(g):
            if g < groups:
                for n in range(NT):
                    multiply(g, n)

        def scatter(g, n):
            places = dst_sb[:, STARTS[g] * C // 16:STARTS[g + 1] * C // 16]
            nc.vector.tensor_tensor(wins[n][:].indirect(places), ys[g, n][:], gates[g, n][:], MULT)
            if g == groups - 1:
                nc.sync.dma_start(out=out[n * P:(n + 1) * P, :], in_=wins[n][:])

        gather(0, E)
        for h in range(2):
            halved = stream.tile([P, GROUPS[0], HALF, J], BF16, name="w_halved", bufs=2, align_bytes=64)
            for e in range(GROUPS[0]):
                copy((e, h) in ((1, 1), (2, 1)), halved[:, e], w_raw[e, h])
            codes = stream.tile([P, GROUPS[0] * HALF], U32, name="w_half_codes", bufs=2, align_bytes=64)
            scales = stream.tile([P, GROUPS[0] * HALF], U8, name="w_half_scales", bufs=2, align_bytes=64)
            quantize(halved[:].rearrange("p e n j -> p (e n) j"), codes[:], scales[:])
            for e in range(GROUPS[0]):
                for m in range(2):
                    c0 = e * HALF + m * P
                    coded_w[e, 2 * h + m] = codes[:, c0:c0 + P], scales[:, c0:c0 + P]
            for n in range(2 * h, 2 * h + 2):
                multiply(0, n)
        stage_group(1)
        for g in range(groups):
            stage_quantize(g + 1)
            stage_multiply(g + 1)
            for n in range(NT):
                scatter(g, n)
            stage_group(g + 2)
